import numpy as np
CORES = [14,30,46,142,158,174,270,286,302,398,414,430]
N = 12
HOST = [c // 128 for c in CORES]
HS = sorted(set(HOST)); H = len(HS)
R, T = 4096, 1024
def entries(a): return a.T.reshape(-1)
def pack(v, P): return np.ascontiguousarray(np.asarray(v, np.int32).reshape(-1, P).T)
def lists(rng, how):
    A = np.array(HOST); L = [rng.permutation(N * R)[:T] for h in HS]
    if how == "away": L = [R * int(rng.choice(np.flatnonzero(A != h))) + rng.permutation(R)[:T] for h in HS]
    if how == "edge": E = R * np.arange(N); E = np.concatenate([E, E + R - 1]); F = np.setdiff1d(np.arange(N * R), E); L = [rng.permutation(np.concatenate([E, rng.permutation(F)[:T - 2 * N]])) for h in HS]
    if how == "home": O = np.repeat(A, R); L = [rng.permutation(np.flatnonzero(O == h))[:T] for h in HS]
    if how == "hotrank": z = R * int(rng.integers(N)); L = [z + rng.permutation(R)[:T] for h in HS]
    if how == "meet": L = [rng.permutation(L[0]) for h in HS]
    return {"idx": np.stack([pack(L[HS.index(HOST[r])], 16) for r in range(N)])}
def setup_inputs(rng):
    return dict({"g": rng.standard_normal((N, 128, T), dtype=np.float32)}, **lists(rng, "uniform"))
def setup_inputs_away(rng):
    d = setup_inputs(rng); d.update(lists(rng, "away"))
    for k in ("g",): d[k] = (d[k].astype(np.float32) * 1024.0).astype(d[k].dtype)
    return d
def setup_inputs_edge(rng):
    d = setup_inputs(rng); d.update(lists(rng, "edge"))
    for k in ("g",): d[k] = (d[k].astype(np.float32) * (1 / 1024.0)).astype(d[k].dtype)
    return d
def setup_inputs_home(rng):
    d = setup_inputs(rng); d.update(lists(rng, "home"))
    return d
def setup_inputs_hotrank(rng):
    d = setup_inputs(rng); d.update(lists(rng, "hotrank"))
    return d
def setup_inputs_meet(rng):
    d = setup_inputs(rng); d.update(lists(rng, "meet"))
    return d
def check_inputs(x):
    bad = []
    if x["idx"].min() < 0 or x["idx"].max() >= N * R: bad.append("idx out of range")
    if any(len(np.unique(a)) != a.size for a in x["idx"]): bad.append("a number stands twice in a list")
    if any(HOST[p] == HOST[s] and not np.array_equal(x["idx"][p], x["idx"][s]) for p in range(N) for s in range(p)): bad.append("two ranks of one host hold different lists")
    return bad
def reference(g, idx):
    S = np.zeros((128, N * R))
    for q in range(N):
        I = entries(idx[q]); S[:, I] += g[q].astype(np.float64)
    return {"y": np.stack([S[:, R * r:R * r + R] for r in range(N)]).astype(np.float32)}

@@ -1,0 +1,412 @@
+from concourse.bass import DstId, RemoteDMATransfer
+from concourse.mybir import AluOpType as A, AxisListType, ActivationFunctionType as F
+
+NPIECE = 12
+PW = 86
+SLOT = NPIECE * PW
+W0 = 8
+Z = W0 - 1
+NB, BW = 8, 512
+
+SCRATCH = {
+    "gb": ("sbuf", [128, SLOT], "float32"),
+    "win": ("sbuf", [128, W0 + 4 * SLOT], "float32"),
+    "yb": ("sbuf", [128, 4096], "float32"),
+    "li": ("sbuf", [128, 32], "int32"),
+    "hi": ("sbuf", [128, 32], "int32"),
+    "lo": ("sbuf", [128, 32], "int32"),
+    "hic": ("sbuf", [128, 32], "float32"),
+    "lof": ("sbuf", [128, 32], "float32"),
+    "hiu": ("sbuf", [128, 32], "uint16"),
+    "ohr": ("sbuf", [128, 32 * 256], "float16"),
+    "ohl": ("sbuf", [128, 32 * 128], "float16"),
+    "i256": ("sbuf", [128, 256], "bfloat16"),
+    "im16": ("sbuf", [128, 128], "bfloat16"),
+    "id16": ("sbuf", [128, 128], "bfloat16"),
+    "im8": ("sbuf", [128, 64], "bfloat16"),
+    "ip": ("sbuf", [128, 1], "int32"),
+    "ie": ("sbuf", [128, 8], "int32"),
+    "pmi": ("sbuf", [128, 1], "int32"),
+    "pgi": ("sbuf", [128, 1], "int32"),
+    "pm": ("sbuf", [128, 1], "float32"),
+    "pg": ("sbuf", [128, 1], "float32"),
+    "pg112": ("sbuf", [128, 1], "float32"),
+    "ev": ("sbuf", [128, 8], "float32"),
+    "ma": ("sbuf", [128, 16], "bfloat16"),
+    "bk": ("sbuf", [128, 128], "bfloat16"),
+    "l2": ("sbuf", [128, 128], "float32"),
+    "ee": ("sbuf", [128, 64], "float32"),
+    "mq": ("sbuf", [128, 64], "float32"),
+    "rm": ("sbuf", [128, 384], "bfloat16"),
+    "msk": ("sbuf", [128, 384], "float32"),
+    "gt": ("sbuf", [128, 384], "float32"),
+    "xt": ("sbuf", [128, 384], "float32"),
+    "r2": ("sbuf", [128, 192], "float32"),
+    "off": ("sbuf", [128, 192], "uint16"),
+    "tw0": ("sbuf", [128, 264], "float32"),
+    "tw1": ("sbuf", [128, 264], "float32"),
+    "tw2": ("sbuf", [128, 264], "float32"),
+    "tw3": ("sbuf", [128, 264], "float32"),
+    "tu": ("sbuf", [128, 768], "float32"),
+    "tv": ("sbuf", [128, 768], "float32"),
+    "pos": ("sbuf", [128, 256], "uint16"),
+    "rsb": ("sbuf", [128, 3 * 88], "float32"),
+    "s1": ("sbuf", [128, 88], "float32"),
+    "sm": ("sbuf", [128, 88], "float32"),
+    "cb": ("sbuf", [128, 88], "float32"),
+    "lst": ("sbuf", [128, 8], "int32"),
+    "p0": ("psum", [128, 512], "float32"),
+    "p1": ("psum", [128, 512], "float32"),
+    "p2": ("psum", [128, 512], "float32"),
+    "p3": ("psum", [128, 512], "float32"),
+    "cl": ("psum", [128, 512], "float32"),
+    "cld": ("psum", [128, 512], "float32"),
+    "o1": ("psum", [128, 512], "float32"),
+    "o2": ("psum", [128, 512], "float32"),
+}
+SEMAPHORES = (["loc", "ldl", "ldg", "gi", "pad", "cst", "vs", "prep", "prepd", "rm", "rmd", "cl", "cld", "xt", "xtd", "m1", "m1d",
+               "r2", "r2d", "m2", "m2d", "of", "mrg", "st", "l1", "l2", "l3", "v01", "v2", "v3", "lst", "rs", "hs", "sum", "cab"]
+              + ["oh%d" % s for s in range(4)] + ["pt%d" % s for s in range(4)] + ["yd%d" % b for b in range(NB)])
+
+
+def engines(mask):
+    return [b for b in range(16) if mask >> b & 1]
+
+
+def bits(es):
+    return sum(1 << b for b in es)
+
+
+_PLAN = {}
+
+
+def plan(T, topo):
+    if not _PLAN:
+        cores = list(T.cores)
+        spot = {(topo.host(c), topo.chip(c)): [] for c in cores}
+        for c in range(128 * 4):
+            if (topo.host(c), topo.chip(c)) in spot:
+                spot[topo.host(c), topo.chip(c)].append(c)
+        helpers = []
+        for c in cores:
+            on = spot[topo.host(c), topo.chip(c)]
+            helpers.append([[x for x in on[2 * u:2 * u + 2] if x not in cores][0] for u in range(len(on) // 2)])
+        _PLAN["helpers"] = helpers
+    return _PLAN["helpers"]
+
+
+def rank_program(g, core, T, topo):
+    cores = list(T.cores)
+    helpers = plan(T, topo)
+    hosts = [topo.host(c) for c in cores]
+
+    def here(r, hst):
+        return [q for q in range(len(cores)) if hosts[q] == hst and topo.chip(cores[q]) == topo.chip(cores[r])][0]
+
+    def rack_peer(r):
+        return [here(r, h) for h in sorted(set(hosts)) if h != hosts[r] and topo.rack(h) == topo.rack(hosts[r])][0]
+
+    def cable_peer(r):
+        return [q for q in (here(r, h) for h in sorted(set(hosts)) if topo.rack(h) != topo.rack(hosts[r]))
+                if topo.may_write(cores[r], cores[q])][0]
+
+    def dst(d):
+        rid, pid = topo.addr(d, core)
+        return DstId(rid=rid, pnc=pid)
+
+    def same_chip(d):
+        return (topo.host(d), topo.chip(d)) == (topo.host(core), topo.chip(core))
+
+    def xfer(src, pairs, es, sem):
+        return RemoteDMATransfer(dst_ids=[dst(d) for d, _ in pairs], dma_engine_mask=bits(es), remote_sem=sem,
+                                 srcs=[src], dsts=[ap for _, ap in pairs], alu_op=0)
+
+    sem = T.sem
+    rank = T.rank_of(core)
+    NON = 4
+    NOFF = 8
+    if rank is not None:
+        mates = [r for r in range(len(cores)) if hosts[r] == hosts[rank]]
+        run_rank(g, core, rank, mates, helpers, T, topo, xfer, same_chip, NON, NOFF)
+        return
+    own = [(r, u) for r in range(len(cores)) for u in range(4) if helpers[r][u] == core]
+    if not own:
+        return
+    r, u = own[0]
+    mates = [q for q in range(len(cores)) if hosts[q] == hosts[r]]
+    others = [q for q in range(len(cores)) if topo.rack(hosts[q]) == topo.rack(hosts[r]) and q not in mates]
+    k = 4 * mates.index(r) + u
+    R, C = rack_peer(r), cable_peer(r)
+    off_es = engines(topo.mask(core, cores[R]))
+    on_es = [e for e in engines(topo.mask(core, cores[r])) if e not in off_es]
+    nloc = 0
+
+    def send(ts):
+        g.remote_dma_fused(ts, local_sem=sem.loc)
+
+    g.wait_ge(sem.lst, 8 if u == 3 else 4)
+    L = T.lst[:, :]
+    if u == 0:
+        send([xfer(L, [(cores[R], T.li[:, 8:16])], off_es, sem.l1)])
+    elif u == 1:
+        send([xfer(L, [(cores[C], T.li[:, 16:24])], off_es, sem.l2)])
+    elif u == 2:
+        send([xfer(L, [(helpers[C][3], T.lst[:, :])], off_es, sem.lst)])
+    else:
+        send([xfer(L, [(cores[R], T.li[:, 24:32])], off_es, sem.l3)])
+    nloc += len(off_es)
+    g.vector.wait_ge(sem.rs, 3)
+    g.vector.tensor_tensor(out=T.s1[:, 0:PW], in0=T.rsb[:, 0:PW], in1=T.rsb[:, 88:88 + PW], op=A.add).then_inc(sem.hs, 1)
+    g.vector.wait_ge(sem.hs, 1)
+    g.vector.tensor_tensor(out=T.sm[:, 0:PW], in0=T.s1[:, 0:PW], in1=T.rsb[:, 176:176 + PW], op=A.add).then_inc(sem.sum, 1)
+    g.wait_ge(sem.sum, 1)
+
+    def at(slot):
+        a = W0 + SLOT * slot + PW * k
+        return T.win[:, a:a + PW]
+
+    S = T.sm[:, 0:PW]
+    send([xfer(S, [(helpers[C][u], T.cb[:, 0:PW])], off_es, sem.cab)])
+    send([xfer(S, [(cores[q], at(0)) for q in mates if q != r] + [(cores[q], at(1)) for q in others], off_es, sem.v01),
+          xfer(S, [(cores[r], at(0))], on_es[:NON], sem.v01)])
+    g.wait_ge(sem.cab, len(off_es))
+    B = T.cb[:, 0:PW]
+    send([xfer(B, [(cores[q], at(2)) for q in mates if q != r], off_es, sem.v2),
+          xfer(B, [(cores[r], at(2))], on_es[:NON], sem.v2)])
+    send([xfer(B, [(cores[q], at(3)) for q in others], off_es, sem.v3)])
+    nloc += 4 * len(off_es) + 2 * NON
+    g.wait_ge(sem.loc, nloc)
+
+
+def run_rank(g, core, rank, mates, helpers, T, topo, xfer, same_chip, NON, NOFF):
+    sem = T.sem
+    V, S, P, Q = g.vector, g.scalar, g.tensor, g.sync
+    S.dma_start(T.gb[:, 0:1024], T.g[:, :]).then_inc(sem.ldg, 16)
+    for i in range(8):
+        Q.dma_start(T.li[16 * i:16 * i + 16, 0:8], T.idx[:, 8 * i:8 * i + 8]).then_inc(sem.ldl, 16)
+
+    def iota(name, pattern, base, mult):
+        g.iota(T[name][:, :], pattern, base, mult, allow_small_or_imprecise_dtypes=True).then_inc(sem.gi, 1)
+
+    iota("ip", [[0, 1]], 0, 1)
+    iota("ie", [[16, 8]], 1, 1)
+    iota("im16", [[0, 8], [1, 16]], 0, 0)
+    iota("i256", [[1, 256]], 1, 0)
+    iota("id16", [[1, 8], [0, 16]], 0, 0)
+    iota("im8", [[0, 8], [1, 8]], 0, 0)
+    hs = helpers[rank]
+    far = [h for q in mates if q != rank for h in helpers[q]]
+    off_es = engines(topo.mask(core, far[0]))
+    on_es = [e for e in engines(topo.mask(core, hs[0])) if e not in off_es]
+    les = (off_es + on_es)[:12]
+    g.wait_ge(sem.ldl, 128)
+    g.remote_dma_fused([xfer(T.li[:, 0:8], [(hs[u], T.lst[:, :])], les[4 * u:4 * u + 4], sem.lst) for u in range(3)],
+                       local_sem=sem.loc)
+    g.wait_ge(sem.ldg, 16)
+    g.wait_ge(sem.pad, 1)
+    ts, i_off, i_on = [], 0, 0
+    me = mates.index(rank)
+    for m, q in enumerate(mates):
+        for u in range(4):
+            k = 4 * m + u
+            if q == rank:
+                e, i_on = on_es[i_on], i_on + 1
+            else:
+                e, i_off = off_es[i_off], i_off + 1
+            ts.append(xfer(T.gb[:, PW * k:PW * k + PW], [(helpers[q][u], T.rsb[:, 88 * me:88 * me + PW])], [e], sem.rs))
+    g.remote_dma_fused(ts, local_sem=sem.loc)
+    g.wait_ge(sem.loc, 24)
+
+    issued, waited = {}, {}
+
+    def v(call, name="vs", **kw):
+        call(**kw).then_inc(sem[name], 1)
+        issued[name] = issued.get(name, 0) + 1
+
+    def vsync():
+        for n in issued:
+            if waited.get(n, 0) < issued[n]:
+                V.wait_ge(sem[n], issued[n])
+                waited[n] = issued[n]
+
+    def memset(ap, name="vs"):
+        V.memset(ap, 0.0).then_inc(sem[name], 1)
+        issued[name] = issued.get(name, 0) + 1
+
+    def ts_(out, in0, s1, op0, s2=None, op1=None, name="vs"):
+        if op1 is None:
+            v(V.tensor_scalar, name, out=out, in0=in0, scalar1=s1, scalar2=None, op0=op0)
+        else:
+            v(V.tensor_scalar, name, out=out, in0=in0, scalar1=s1, scalar2=s2, op0=op0, op1=op1)
+
+    def tt(out, in0, in1, op, name="vs"):
+        v(V.tensor_tensor, name, out=out, in0=in0, in1=in1, op=op)
+
+    def cp(out, in_, name="vs"):
+        v(V.tensor_copy, name, out=out, in_=in_)
+
+    memset(T.gb[:, 1024:SLOT], "pad")
+    memset(T.win[:, 0:W0])
+    for s in range(3):
+        memset(T["tw%d" % s][:, 0:1])
+        memset(T["tw%d" % s][:, 257:264])
+    V.wait_ge(sem.gi, 6)
+    ts_(T.pmi[:, :], T.ip[:, :], 15, A.bitwise_and)
+    ts_(T.pgi[:, :], T.ip[:, :], 4, A.arith_shift_right)
+    vsync()
+    cp(T.pm[:, :], T.pmi[:, :])
+    cp(T.pg[:, :], T.pgi[:, :])
+    ts_(T.pg112[:, :], T.pgi[:, :], 112.0, A.mult)
+    vsync()
+    ts_(T.ev[:, :], T.ie[:, :], T.pg112[:, :], A.add)
+    ts_(T.ma[:, :], T.im16[:, 0:16], T.pm[:, :], A.is_equal, name="cst")
+    ts_(T.bk[:, :], T.id16[:, :], T.pg[:, :], A.is_equal, name="cst")
+    ts_(T.ee[:, :], T.id16[:, 0:128:2], T.pg[:, :], A.is_equal, name="cst")
+    ts_(T.l2[:, :], T.im16[:, :], T.pm[:, :], A.is_equal, name="cst")
+    ts_(T.mq[:, :], T.im8[:, :], T.pg[:, :], A.is_equal, name="cst")
+
+    def prep(s, e, name):
+        a, b = 8 * s, 8 * e
+        ts_(T.lo[:, a:b], T.li[:, a:b], 15, A.bitwise_and)
+        ts_(T.hi[:, a:b], T.li[:, a:b], 4, A.arith_shift_right)
+        vsync()
+        cp(T.lof[:, a:b], T.lo[:, a:b], name)
+        ts_(T.hic[:, a:b], T.hi[:, a:b], float(256 * rank - 1), A.subtract, 0.0, A.max)
+        vsync()
+        if s > 0:
+            ts_(T.hiu[:, a:b], T.hic[:, a:b], 257.0, A.min)
+
+    def onehots(s):
+        for q in range(8):
+            c = 8 * s + q
+            ts_(T.ohl[:, 128 * c:128 * c + 128], T.im16[:, :], T.lof[:, c:c + 1], A.is_equal, T.ev[:, q:q + 1], A.mult, "oh%d" % s)
+            ts_(T.ohr[:, 256 * c:256 * c + 256], T.i256[:, :], T.hic[:, c:c + 1], A.is_equal, name="oh%d" % s)
+
+    def table(s):
+        p = T["p%d" % s][:, 0:256]
+        out = T["tw%d" % s][:, 1:257]
+        V.wait_ge(sem["pt%d" % s], 8)
+        if s == 0:
+            cp(out, p)
+            return
+        a = 256 * (s - 1)
+        ts_(T.tu[:, a:a + 256], p, 0.0, A.is_gt, float(SLOT * s), A.mult)
+        vsync()
+        tt(T.tv[:, a:a + 256], T.tu[:, a:a + 256], p, A.add)
+        vsync()
+        tt(out, T.tv[:, a:a + 256], T["tw%d" % (s - 1)][:, 1:257], A.max)
+
+    def lookup(s):
+        c = 128 * (s - 1)
+        cp(T.gt[:, c:c + 128], T["tw%d" % (s - 1)][:, 0:258].indirect(T.hiu[:, 8 * s:8 * s + 8]))
+
+    V.wait_ge(sem.ldl, 128)
+    prep(0, 1, "vs")
+    vsync()
+    onehots(0)
+    V.wait_ge(sem.l1, 8)
+    V.wait_ge(sem.l2, 8)
+    prep(1, 3, "prep")
+    vsync()
+    onehots(1)
+    onehots(2)
+    table(0)
+    V.wait_ge(sem.cl, 1)
+    ts_(T.msk[:, 0:256], T.cl[:, 0:256], T.pm[:, :], A.is_equal)
+    vsync()
+    lookup(1)
+    table(1)
+    vsync()
+    lookup(2)
+    vsync()
+    tt(T.xt[:, 0:256], T.gt[:, 0:256], T.msk[:, 0:256], A.mult, "xt")
+    table(2)
+    V.wait_ge(sem.m1, 2)
+    tt(T.r2[:, 0:64], T.o1[:, 0:64], T.mq[:, :], A.mult, "r2")
+    tt(T.r2[:, 64:128], T.o1[:, 64:128], T.mq[:, :], A.mult, "r2")
+    V.wait_ge(sem.l3, 8)
+    prep(3, 4, "prepd")
+    vsync()
+    lookup(3)
+    onehots(3)
+    V.wait_ge(sem.m2, 1)
+    cp(T.off[:, 0:128], T.o2[:, 0:128], "of")
+    V.wait_ge(sem.cld, 1)
+    ts_(T.msk[:, 256:384], T.cld[:, 0:128], T.pm[:, :], A.is_equal)
+    vsync()
+    tt(T.xt[:, 256:384], T.gt[:, 256:384], T.msk[:, 256:384], A.mult, "xtd")
+    table(3)
+    V.wait_ge(sem.m1d, 1)
+    tt(T.r2[:, 128:192], T.o1[:, 128:192], T.mq[:, :], A.mult, "r2d")
+    vsync()
+    cp(T.pos[:, :], T.tw3[:, 1:257])
+    V.wait_ge(sem.m2d, 1)
+    cp(T.off[:, 128:192], T.o2[:, 128:192])
+    vsync()
+
+    near = 4 * NON + 4 * (len(mates) - 1) * NOFF
+    other = 4 * len(mates) * NOFF
+
+    def merge(s, name):
+        a = W0 + SLOT * s
+        tt(T.win[:, a:a + 1024], T.win[:, Z:a].indirect(T.off[:, 64 * (s - 1):64 * s]), T.win[:, a:a + 1024], A.add, name)
+
+    V.wait_ge(sem.v01, near + other)
+    merge(1, "vs")
+    V.wait_ge(sem.v2, near)
+    vsync()
+    merge(2, "vs")
+    V.wait_ge(sem.v3, other)
+    vsync()
+    merge(3, "mrg")
+    vsync()
+    end = W0 + 4 * SLOT
+
+    def src(b):
+        return T.win[:, Z:end].indirect(T.pos[:, 32 * b:32 * b + 32])
+
+    for b in range(0, NB, 2):
+        V.tensor_copy(out=T.yb[:, BW * b:BW * b + BW], in_=src(b)).then_inc(sem["yd%d" % b], 1)
+
+    S.wait_ge(sem.cst, 5)
+    S.wait_ge(sem.prep, 1)
+    for n in range(16):
+        S.activation(out=T.rm[:, 16 * n:16 * n + 16], in_=T.ma[:, :], func=F.Copy, scale=T.lof[:, 8 + n:9 + n]).then_inc(sem.rm, 1)
+    S.wait_ge(sem.prepd, 1)
+    for n in range(16, 24):
+        S.activation(out=T.rm[:, 16 * n:16 * n + 16], in_=T.ma[:, :], func=F.Copy, scale=T.lof[:, 8 + n:9 + n]).then_inc(sem.rmd, 1)
+    S.wait_ge(sem.mrg, 1)
+    for b in range(1, NB, 2):
+        S.activation(out=T.yb[:, BW * b:BW * b + BW], in_=src(b), func=F.Copy).then_inc(sem["yd%d" % b], 1)
+
+    def positions(s):
+        P.wait_ge(sem["oh%d" % s], 16)
+        for q in range(8):
+            c = 8 * s + q
+            P.matmul(T["p%d" % s][:, 0:256], T.ohl[:, 128 * c:128 * c + 128], T.ohr[:, 256 * c:256 * c + 256],
+                     q == 0, q == 7).then_inc(sem["pt%d" % s], 1)
+
+    P.wait_ge(sem.cst, 5)
+    positions(0)
+    P.wait_ge(sem.rm, 16)
+    P.matmul(T.cl[:, 0:256], T.bk[:, :], T.rm[:, 0:256], True, True).then_inc(sem.cl, 1)
+    positions(1)
+    positions(2)
+    P.wait_ge(sem.xt, 1)
+    for s in range(2):
+        P.matmul(T.o1[:, 64 * s:64 * s + 64], T.xt[:, 128 * s:128 * s + 128], T.ee[:, :], True, True).then_inc(sem.m1, 1)
+    P.wait_ge(sem.r2, 2)
+    P.matmul(T.o2[:, 0:128], T.l2[:, :], T.r2[:, 0:128], True, True).then_inc(sem.m2, 1)
+    P.wait_ge(sem.rmd, 8)
+    P.matmul(T.cld[:, 0:128], T.bk[:, :], T.rm[:, 256:384], True, True).then_inc(sem.cld, 1)
+    positions(3)
+    P.wait_ge(sem.xtd, 1)
+    P.matmul(T.o1[:, 128:192], T.xt[:, 256:384], T.ee[:, :], True, True).then_inc(sem.m1d, 1)
+    P.wait_ge(sem.r2d, 1)
+    P.wait_ge(sem.of, 1)
+    P.matmul(T.o2[:, 128:192], T.l2[:, :], T.r2[:, 128:192], True, True).then_inc(sem.m2d, 1)
+
+    for b in range(NB):
+        Q.wait_ge(sem["yd%d" % b], 1)
+        Q.dma_start(T.y[:, BW * b:BW * b + BW], T.yb[:, BW * b:BW * b + BW]).then_inc(sem.st, 16)
+    Q.wait_ge(sem.st, 16 * NB)

@@ -6,24 +6,46 @@ PW = 86
 SLOT = NPIECE * PW
 W0 = 8
 Z = W0 - 1
-NB, BW = 8, 512
+BLOCKS = [256, 256, 512, 512, 640, 640, 640, 640]
+NON = 4
+TB = 272
+QS = 6
 
 SCRATCH = {
     "gb": ("sbuf", [128, SLOT], "float32"),
     "win": ("sbuf", [128, W0 + 4 * SLOT], "float32"),
     "yb": ("sbuf", [128, 4096], "float32"),
-    "li": ("sbuf", [128, 32], "int32"),
-    "hi": ("sbuf", [128, 32], "int32"),
-    "lo": ("sbuf", [128, 32], "int32"),
-    "hic": ("sbuf", [128, 32], "float32"),
-    "lof": ("sbuf", [128, 32], "float32"),
+    "tin": ("sbuf", [128, 3 * TB], "float32"),
+    "mkin": ("sbuf", [128, 384], "bfloat16"),
     "hiu": ("sbuf", [128, 32], "uint16"),
-    "ohr": ("sbuf", [128, 32 * 256], "float16"),
-    "ohl": ("sbuf", [128, 32 * 128], "float16"),
+    "ee": ("sbuf", [128, 64], "float32"),
+    "l2": ("sbuf", [128, 128], "float32"),
+    "im8": ("sbuf", [128, 192], "bfloat16"),
+    "mq": ("sbuf", [128, 192], "float32"),
+    "gt": ("sbuf", [128, 384], "float32"),
+    "xt": ("sbuf", [128, 384], "float32"),
+    "r2": ("sbuf", [128, 192], "float32"),
+    "off": ("sbuf", [128, 192], "uint16"),
+    "tw1": ("sbuf", [128, 264], "float32"),
+    "tw2": ("sbuf", [128, 264], "float32"),
+    "tw3": ("sbuf", [128, 264], "float32"),
+    "pos": ("sbuf", [128, 256], "uint16"),
+    "li": ("sbuf", [128, 16], "int32"),
+    "hi": ("sbuf", [128, 8], "int32"),
+    "lo": ("sbuf", [128, 8], "int32"),
+    "lof": ("sbuf", [128, 8], "float32"),
+    "tb": ("sbuf", [128, TB], "float32"),
+    "tu": ("sbuf", [128, 256], "float32"),
+    "ohr": ("sbuf", [128, 8 * 256], "float16"),
+    "ohl": ("sbuf", [128, 8 * 128], "float16"),
+    "ab": ("sbuf", [128, 2 * 256], "bfloat16"),
+    "lom": ("sbuf", [128, 8], "int32"),
+    "lomf": ("sbuf", [128, 8], "float32"),
+    "rm": ("sbuf", [128, 128], "bfloat16"),
+    "mk": ("sbuf", [128, 128], "bfloat16"),
     "i256": ("sbuf", [128, 256], "bfloat16"),
     "im16": ("sbuf", [128, 128], "bfloat16"),
     "id16": ("sbuf", [128, 128], "bfloat16"),
-    "im8": ("sbuf", [128, 64], "bfloat16"),
     "ip": ("sbuf", [128, 1], "int32"),
     "ie": ("sbuf", [128, 8], "int32"),
     "pmi": ("sbuf", [128, 1], "int32"),
@@ -34,39 +56,18 @@ SCRATCH = {
     "ev": ("sbuf", [128, 8], "float32"),
     "ma": ("sbuf", [128, 16], "bfloat16"),
     "bk": ("sbuf", [128, 128], "bfloat16"),
-    "l2": ("sbuf", [128, 128], "float32"),
-    "ee": ("sbuf", [128, 64], "float32"),
-    "mq": ("sbuf", [128, 64], "float32"),
-    "rm": ("sbuf", [128, 384], "bfloat16"),
-    "msk": ("sbuf", [128, 384], "float32"),
-    "gt": ("sbuf", [128, 384], "float32"),
-    "xt": ("sbuf", [128, 384], "float32"),
-    "r2": ("sbuf", [128, 192], "float32"),
-    "off": ("sbuf", [128, 192], "uint16"),
-    "tw0": ("sbuf", [128, 264], "float32"),
-    "tw1": ("sbuf", [128, 264], "float32"),
-    "tw2": ("sbuf", [128, 264], "float32"),
-    "tw3": ("sbuf", [128, 264], "float32"),
-    "tu": ("sbuf", [128, 768], "float32"),
-    "tv": ("sbuf", [128, 768], "float32"),
-    "pos": ("sbuf", [128, 256], "uint16"),
     "rsb": ("sbuf", [128, 3 * 88], "float32"),
     "s1": ("sbuf", [128, 88], "float32"),
     "sm": ("sbuf", [128, 88], "float32"),
     "cb": ("sbuf", [128, 88], "float32"),
-    "lst": ("sbuf", [128, 8], "int32"),
-    "p0": ("psum", [128, 512], "float32"),
-    "p1": ("psum", [128, 512], "float32"),
-    "p2": ("psum", [128, 512], "float32"),
-    "p3": ("psum", [128, 512], "float32"),
+    "pp": ("psum", [128, 512], "float32"),
     "cl": ("psum", [128, 512], "float32"),
-    "cld": ("psum", [128, 512], "float32"),
     "o1": ("psum", [128, 512], "float32"),
     "o2": ("psum", [128, 512], "float32"),
 }
-SEMAPHORES = (["loc", "ldl", "ldg", "gi", "pad", "cst", "vs", "prep", "prepd", "rm", "rmd", "cl", "cld", "xt", "xtd", "m1", "m1d",
-               "r2", "r2d", "m2", "m2d", "of", "mrg", "st", "l1", "l2", "l3", "v01", "v2", "v3", "lst", "rs", "hs", "sum", "cab"]
-              + ["oh%d" % s for s in range(4)] + ["pt%d" % s for s in range(4)] + ["yd%d" % b for b in range(NB)])
+SEMAPHORES = (["loc", "ldl", "ldg", "gi", "pad", "cst", "vs", "prep", "prepm", "rm", "cl", "xt", "m1", "r2", "m2", "mrg", "st",
+               "lst", "lst2", "tin", "mkin", "tab", "tabm", "oha", "ohb", "abs", "ohs", "pt", "v01", "v2", "v3", "rs", "sum",
+               "cab"] + ["yd%d" % b for b in range(len(BLOCKS))])
 
 
 def engines(mask):
@@ -87,17 +88,156 @@ def plan(T, topo):
         for c in range(128 * 4):
             if (topo.host(c), topo.chip(c)) in spot:
                 spot[topo.host(c), topo.chip(c)].append(c)
-        helpers = []
+        helpers, indexers = [], []
         for c in cores:
             on = spot[topo.host(c), topo.chip(c)]
-            helpers.append([[x for x in on[2 * u:2 * u + 2] if x not in cores][0] for u in range(len(on) // 2)])
-        _PLAN["helpers"] = helpers
-    return _PLAN["helpers"]
+            hs = [[x for x in on[2 * u:2 * u + 2] if x not in cores][0] for u in range(len(on) // 2)]
+            helpers.append(hs)
+            indexers.append([x for x in on if x not in hs and x not in cores])
+        _PLAN["h"], _PLAN["x"] = helpers, indexers
+    return _PLAN["h"], _PLAN["x"]
+
+
+def vector_queue(g, T):
+    V, sem = g.vector, T.sem
+    issued, waited = {}, {}
+
+    def note(ins, name):
+        ins.then_inc(sem[name], 1)
+        issued[name] = issued.get(name, 0) + 1
+
+    def sync():
+        for n in issued:
+            if waited.get(n, 0) < issued[n]:
+                V.wait_ge(sem[n], issued[n])
+                waited[n] = issued[n]
+
+    def fill(ap, name="vs"):
+        note(V.memset(ap, 0.0), name)
+
+    def ts(out, in0, s1, op0, s2=None, op1=None, name="vs"):
+        if op1 is None:
+            note(V.tensor_scalar(out=out, in0=in0, scalar1=s1, scalar2=None, op0=op0), name)
+        else:
+            note(V.tensor_scalar(out=out, in0=in0, scalar1=s1, scalar2=s2, op0=op0, op1=op1), name)
+
+    def tt(out, in0, in1, op, name="vs"):
+        note(V.tensor_tensor(out=out, in0=in0, in1=in1, op=op), name)
+
+    def cp(out, in_, name="vs"):
+        note(V.tensor_copy(out=out, in_=in_), name)
+
+    return sync, fill, ts, tt, cp
+
+
+RAMPS = {"ip": ([[0, 1]], 0, 1), "ie": ([[16, 8]], 1, 1), "im16": ([[0, 8], [1, 16]], 0, 0), "i256": ([[1, 256]], 1, 0),
+         "id16": ([[1, 8], [0, 16]], 0, 0), "im8": ([[0, 24], [1, 8]], 0, 0)}
+KIND = {"rank": (["ip", "im16", "ie", "i256", "id16", "im8"], ["ee", "l2", "mq"]),
+        "index": (["ip", "im16", "ie", "i256"], []),
+        "both": (["ip", "im16", "ie", "i256", "id16"], ["ma", "bk"]),
+        "mask": (["ip", "im16", "id16"], ["ma", "bk"])}
+
+
+def constants(g, T, vq, kind):
+    sync, fill, ts, tt, cp = vq
+    ramps, consts = KIND[kind]
+    for n in ramps:
+        g.iota(T[n][:, :], *RAMPS[n], allow_small_or_imprecise_dtypes=True).then_inc(T.sem.gi, 1)
+    if kind != "mask":
+        fill(T.tb[:, 0:1])
+        fill(T.tb[:, 257:264])
+    g.vector.wait_ge(T.sem.gi, len(ramps))
+    ts(T.pmi[:, :], T.ip[:, :], 15, A.bitwise_and)
+    ts(T.pgi[:, :], T.ip[:, :], 4, A.arith_shift_right)
+    sync()
+    cp(T.pm[:, :], T.pmi[:, :])
+    cp(T.pg[:, :], T.pgi[:, :])
+    if kind != "mask":
+        ts(T.pg112[:, :], T.pgi[:, :], 112.0, A.mult)
+    sync()
+    if kind != "mask":
+        ts(T.ev[:, :], T.ie[:, :], T.pg112[:, :], A.add)
+    make = {"ma": (T.im16[:, 0:16], T.pm),
+            "bk": (T.id16[:, :], T.pg),
+            "ee": (T.id16[:, 0:128:2], T.pg),
+            "l2": (T.im16[:, :], T.pm),
+            "mq": (T.im8[:, :], T.pg)}
+    for n in consts:
+        ts(T[n][:, :], make[n][0], make[n][1][:, :], A.is_equal, name="cst")
+    sync()
+
+
+def mask_list(g, T, vq, L):
+    sync, fill, ts, tt, cp = vq
+    V, S, P, sem = g.vector, g.scalar, g.tensor, T.sem
+    ts(T.lom[:, :], L, 15, A.bitwise_and)
+    sync()
+    cp(T.lomf[:, :], T.lom[:, :], "prepm")
+    S.wait_ge(sem.cst, 2)
+    S.wait_ge(sem.prepm, 1)
+    for q in range(8):
+        S.activation(out=T.rm[:, 16 * q:16 * q + 16], in_=T.ma[:, :], func=F.Copy, scale=T.lomf[:, q:q + 1]).then_inc(sem.rm, 1)
+    P.wait_ge(sem.cst, 2)
+    P.wait_ge(sem.rm, 8)
+    P.matmul(T.cl[:, 0:128], T.bk[:, :], T.rm[:, :], True, True).then_inc(sem.cl, 1)
+    V.wait_ge(sem.cl, 1)
+    ts(T.mk[:, :], T.cl[:, 0:128], T.pm[:, :], A.is_equal, name="tabm")
+    sync()
+
+
+def index_list(g, T, vq, rank, slot):
+    sync, fill, ts, tt, cp = vq
+    V, S, P, sem = g.vector, g.scalar, g.tensor, T.sem
+    L, hic = T.li[:, 8:16], T.tb[:, 264:272]
+    ts(T.hi[:, :], L, 4, A.arith_shift_right)
+    ts(T.lo[:, :], L, 15, A.bitwise_and)
+    sync()
+    ts(hic, T.hi[:, :], float(256 * rank - 1), A.subtract, 0.0, A.max, "prep")
+    cp(T.lof[:, :], T.lo[:, :])
+    sync()
+
+    def hot(q):
+        return T.ohr[:, 256 * q:256 * q + 256]
+
+    for q in range(8):
+        n = "oha" if q < 4 else "ohb"
+        ts(T.ohl[:, 128 * q:128 * q + 128], T.im16[:, :], T.lof[:, q:q + 1], A.is_equal, T.ev[:, q:q + 1], A.mult, n)
+        if q < QS:
+            ts(hot(q), T.i256[:, :], T.tb[:, 264 + q:265 + q], A.is_equal, name=n)
+    S.wait_ge(sem.prep, 1)
+    for q in range(QS, 8):
+        a = 256 * (q - QS)
+        S.activation(out=T.ab[:, a:a + 256], in_=T.i256[:, :], func=F.Abs, bias=T.tb[:, 264 + q:265 + q], scale=-1.0).then_inc(sem.abs, 1)
+    S.wait_ge(sem.abs, 8 - QS)
+    for q in range(QS, 8):
+        a = 256 * (q - QS)
+        S.activation(out=hot(q), in_=T.ab[:, a:a + 256], func=F.Relu, bias=1.0, scale=-1.0).then_inc(sem.ohs, 1)
+
+    def mm(q):
+        P.matmul(T.pp[:, 0:256], T.ohl[:, 128 * q:128 * q + 128], hot(q), q == 0, q == 7).then_inc(sem.pt, 1)
+
+    P.wait_ge(sem.oha, 8)
+    for q in range(4):
+        mm(q)
+    P.wait_ge(sem.ohb, 4 + QS - 4)
+    for q in range(4, QS):
+        mm(q)
+    P.wait_ge(sem.ohs, 8 - QS)
+    for q in range(QS, 8):
+        mm(q)
+    V.wait_ge(sem.pt, 8)
+    if slot == 0:
+        cp(T.tb[:, 1:257], T.pp[:, 0:256], "tab")
+    else:
+        ts(T.tu[:, :], T.pp[:, 0:256], 0.0, A.is_gt, float(SLOT * slot), A.mult)
+        sync()
+        tt(T.tb[:, 1:257], T.tu[:, :], T.pp[:, 0:256], A.add, "tab")
+    sync()
 
 
 def rank_program(g, core, T, topo):
     cores = list(T.cores)
-    helpers = plan(T, topo)
+    helpers, indexers = plan(T, topo)
     hosts = [topo.host(c) for c in cores]
 
     def here(r, hst):
@@ -114,22 +254,42 @@ def rank_program(g, core, T, topo):
         rid, pid = topo.addr(d, core)
         return DstId(rid=rid, pnc=pid)
 
-    def same_chip(d):
-        return (topo.host(d), topo.chip(d)) == (topo.host(core), topo.chip(core))
-
     def xfer(src, pairs, es, sem):
         return RemoteDMATransfer(dst_ids=[dst(d) for d, _ in pairs], dma_engine_mask=bits(es), remote_sem=sem,
                                  srcs=[src], dsts=[ap for _, ap in pairs], alu_op=0)
 
     sem = T.sem
     rank = T.rank_of(core)
-    NON = 4
-    NOFF = 8
     if rank is not None:
         mates = [r for r in range(len(cores)) if hosts[r] == hosts[rank]]
-        run_rank(g, core, rank, mates, helpers, T, topo, xfer, same_chip, NON, NOFF)
+        run_rank(g, core, rank, mates, rack_peer(rank), cable_peer(rank), helpers, indexers, T, topo, xfer)
         return
+    vq = vector_queue(g, T)
+    sync, fill, ts, tt, cp = vq
+
+    def send(ts_):
+        g.remote_dma_fused(ts_, local_sem=sem.loc)
+
     own = [(r, u) for r in range(len(cores)) for u in range(4) if helpers[r][u] == core]
+    idx = [(r, s) for r in range(len(cores)) for s in range(3) if indexers[r][s] == core]
+    if idx:
+        r, s = idx[0]
+        R = rack_peer(r)
+        es = engines(topo.mask(core, cores[r]))
+        noff = len(engines(topo.mask(core, cores[R])))
+        constants(g, T, vq, "index" if s else "both")
+        g.vector.wait_ge(sem.lst, noff if s else 4)
+        index_list(g, T, vq, r, s)
+        g.wait_ge(sem.tab, 1)
+        g.wait_ge(sem.prep, 1)
+        send([xfer(T.tb[:, :], [(cores[r], T.tin[:, TB * s:TB * s + TB])], es[:8], sem.tin)])
+        if s == 0:
+            g.vector.wait_ge(sem.lst2, noff)
+            mask_list(g, T, vq, T.li[:, 0:8])
+            g.wait_ge(sem.tabm, 1)
+            send([xfer(T.mk[:, :], [(cores[r], T.mkin[:, 128:256])], es[:8], sem.mkin)])
+        g.wait_ge(sem.loc, 8 if s else 16)
+        return
     if not own:
         return
     r, u = own[0]
@@ -139,26 +299,25 @@ def rank_program(g, core, T, topo):
     R, C = rack_peer(r), cable_peer(r)
     off_es = engines(topo.mask(core, cores[R]))
     on_es = [e for e in engines(topo.mask(core, cores[r])) if e not in off_es]
-    nloc = 0
+    noff = len(off_es)
+    L = T.li[:, 8:16]
 
-    def send(ts):
-        g.remote_dma_fused(ts, local_sem=sem.loc)
-
-    g.wait_ge(sem.lst, 8 if u == 3 else 4)
-    L = T.lst[:, :]
-    if u == 0:
-        send([xfer(L, [(cores[R], T.li[:, 8:16])], off_es, sem.l1)])
+    if u == 3:
+        g.wait_ge(sem.lst, noff)
+        send([xfer(L, [(cores[R], L)], off_es, sem.lst)])
     elif u == 1:
-        send([xfer(L, [(cores[C], T.li[:, 16:24])], off_es, sem.l2)])
-    elif u == 2:
-        send([xfer(L, [(helpers[C][3], T.lst[:, :])], off_es, sem.lst)])
+        g.wait_ge(sem.lst, 4)
+        send([xfer(L, [(indexers[C][0], T.li[:, 0:8])], off_es, sem.lst2)])
     else:
-        send([xfer(L, [(cores[R], T.li[:, 24:32])], off_es, sem.l3)])
-    nloc += len(off_es)
+        constants(g, T, vq, "mask")
+        g.vector.wait_ge(sem.lst, 4 if u == 0 else noff)
+        mask_list(g, T, vq, L)
+        g.wait_ge(sem.tabm, 1)
+        send([xfer(T.mk[:, :], [(cores[R], T.mkin[:, 128 * u:128 * u + 128])], off_es, sem.mkin)])
     g.vector.wait_ge(sem.rs, 3)
-    g.vector.tensor_tensor(out=T.s1[:, 0:PW], in0=T.rsb[:, 0:PW], in1=T.rsb[:, 88:88 + PW], op=A.add).then_inc(sem.hs, 1)
-    g.vector.wait_ge(sem.hs, 1)
-    g.vector.tensor_tensor(out=T.sm[:, 0:PW], in0=T.s1[:, 0:PW], in1=T.rsb[:, 176:176 + PW], op=A.add).then_inc(sem.sum, 1)
+    tt(T.s1[:, 0:PW], T.rsb[:, 0:PW], T.rsb[:, 88:88 + PW], A.add)
+    sync()
+    tt(T.sm[:, 0:PW], T.s1[:, 0:PW], T.rsb[:, 176:176 + PW], A.add, "sum")
     g.wait_ge(sem.sum, 1)
 
     def at(slot):
@@ -166,45 +325,41 @@ def rank_program(g, core, T, topo):
         return T.win[:, a:a + PW]
 
     S = T.sm[:, 0:PW]
-    send([xfer(S, [(helpers[C][u], T.cb[:, 0:PW])], off_es, sem.cab)])
-    send([xfer(S, [(cores[q], at(0)) for q in mates if q != r] + [(cores[q], at(1)) for q in others], off_es, sem.v01),
+    h = noff // 2
+    send([xfer(S, [(helpers[C][u], T.cb[:, 0:PW])], off_es[:h], sem.cab),
+          xfer(S, [(cores[q], at(0)) for q in mates if q != r] + [(cores[q], at(1)) for q in others], off_es[h:], sem.v01),
           xfer(S, [(cores[r], at(0))], on_es[:NON], sem.v01)])
-    g.wait_ge(sem.cab, len(off_es))
+    g.wait_ge(sem.cab, h)
     B = T.cb[:, 0:PW]
     send([xfer(B, [(cores[q], at(2)) for q in mates if q != r], off_es, sem.v2),
           xfer(B, [(cores[r], at(2))], on_es[:NON], sem.v2)])
     send([xfer(B, [(cores[q], at(3)) for q in others], off_es, sem.v3)])
-    nloc += 4 * len(off_es) + 2 * NON
-    g.wait_ge(sem.loc, nloc)
+    g.wait_ge(sem.loc, 4 * noff + 2 * NON)
 
 
-def run_rank(g, core, rank, mates, helpers, T, topo, xfer, same_chip, NON, NOFF):
+def run_rank(g, core, rank, mates, R, C, helpers, indexers, T, topo, xfer):
     sem = T.sem
     V, S, P, Q = g.vector, g.scalar, g.tensor, g.sync
-    S.dma_start(T.gb[:, 0:1024], T.g[:, :]).then_inc(sem.ldg, 16)
-    for i in range(8):
-        Q.dma_start(T.li[16 * i:16 * i + 16, 0:8], T.idx[:, 8 * i:8 * i + 8]).then_inc(sem.ldl, 16)
-
-    def iota(name, pattern, base, mult):
-        g.iota(T[name][:, :], pattern, base, mult, allow_small_or_imprecise_dtypes=True).then_inc(sem.gi, 1)
-
-    iota("ip", [[0, 1]], 0, 1)
-    iota("ie", [[16, 8]], 1, 1)
-    iota("im16", [[0, 8], [1, 16]], 0, 0)
-    iota("i256", [[1, 256]], 1, 0)
-    iota("id16", [[1, 8], [0, 16]], 0, 0)
-    iota("im8", [[0, 8], [1, 8]], 0, 0)
     hs = helpers[rank]
     far = [h for q in mates if q != rank for h in helpers[q]]
     off_es = engines(topo.mask(core, far[0]))
     on_es = [e for e in engines(topo.mask(core, hs[0])) if e not in off_es]
-    les = (off_es + on_es)[:12]
+    noff = len(off_es)
+    for i in range(8):
+        (Q if i < 4 else S).dma_start(T.li[16 * i:16 * i + 16, 0:8], T.idx[:, 8 * i:8 * i + 8]).then_inc(sem.ldl, 16)
+    Q.dma_start(T.gb[:, 0:1024], T.g[:, :]).then_inc(sem.ldg, 16)
+
     g.wait_ge(sem.ldl, 128)
-    g.remote_dma_fused([xfer(T.li[:, 0:8], [(hs[u], T.lst[:, :])], les[4 * u:4 * u + 4], sem.lst) for u in range(3)],
-                       local_sem=sem.loc)
+    L = T.li[:, 0:8]
+
+    def to(cs):
+        return [(c, T.li[:, 8:16]) for c in cs]
+
+    g.remote_dma_fused([xfer(L, to([helpers[C][3], indexers[R][1], indexers[C][2], helpers[C][2]]), off_es, sem.lst),
+                        xfer(L, to([hs[1], hs[0], indexers[rank][0]]), on_es[0:4], sem.lst)], local_sem=sem.loc)
     g.wait_ge(sem.ldg, 16)
     g.wait_ge(sem.pad, 1)
-    ts, i_off, i_on = [], 0, 0
+    ts_, i_off, i_on = [], 0, 0
     me = mates.index(rank)
     for m, q in enumerate(mates):
         for u in range(4):
@@ -213,200 +368,74 @@ def run_rank(g, core, rank, mates, helpers, T, topo, xfer, same_chip, NON, NOFF)
                 e, i_on = on_es[i_on], i_on + 1
             else:
                 e, i_off = off_es[i_off], i_off + 1
-            ts.append(xfer(T.gb[:, PW * k:PW * k + PW], [(helpers[q][u], T.rsb[:, 88 * me:88 * me + PW])], [e], sem.rs))
-    g.remote_dma_fused(ts, local_sem=sem.loc)
-    g.wait_ge(sem.loc, 24)
+            ts_.append(xfer(T.gb[:, PW * k:PW * k + PW], [(helpers[q][u], T.rsb[:, 88 * me:88 * me + PW])], [e], sem.rs))
+    g.remote_dma_fused(ts_, local_sem=sem.loc)
 
-    issued, waited = {}, {}
-
-    def v(call, name="vs", **kw):
-        call(**kw).then_inc(sem[name], 1)
-        issued[name] = issued.get(name, 0) + 1
-
-    def vsync():
-        for n in issued:
-            if waited.get(n, 0) < issued[n]:
-                V.wait_ge(sem[n], issued[n])
-                waited[n] = issued[n]
-
-    def memset(ap, name="vs"):
-        V.memset(ap, 0.0).then_inc(sem[name], 1)
-        issued[name] = issued.get(name, 0) + 1
-
-    def ts_(out, in0, s1, op0, s2=None, op1=None, name="vs"):
-        if op1 is None:
-            v(V.tensor_scalar, name, out=out, in0=in0, scalar1=s1, scalar2=None, op0=op0)
-        else:
-            v(V.tensor_scalar, name, out=out, in0=in0, scalar1=s1, scalar2=s2, op0=op0, op1=op1)
-
-    def tt(out, in0, in1, op, name="vs"):
-        v(V.tensor_tensor, name, out=out, in0=in0, in1=in1, op=op)
-
-    def cp(out, in_, name="vs"):
-        v(V.tensor_copy, name, out=out, in_=in_)
-
-    memset(T.gb[:, 1024:SLOT], "pad")
-    memset(T.win[:, 0:W0])
-    for s in range(3):
-        memset(T["tw%d" % s][:, 0:1])
-        memset(T["tw%d" % s][:, 257:264])
-    V.wait_ge(sem.gi, 6)
-    ts_(T.pmi[:, :], T.ip[:, :], 15, A.bitwise_and)
-    ts_(T.pgi[:, :], T.ip[:, :], 4, A.arith_shift_right)
-    vsync()
-    cp(T.pm[:, :], T.pmi[:, :])
-    cp(T.pg[:, :], T.pgi[:, :])
-    ts_(T.pg112[:, :], T.pgi[:, :], 112.0, A.mult)
-    vsync()
-    ts_(T.ev[:, :], T.ie[:, :], T.pg112[:, :], A.add)
-    ts_(T.ma[:, :], T.im16[:, 0:16], T.pm[:, :], A.is_equal, name="cst")
-    ts_(T.bk[:, :], T.id16[:, :], T.pg[:, :], A.is_equal, name="cst")
-    ts_(T.ee[:, :], T.id16[:, 0:128:2], T.pg[:, :], A.is_equal, name="cst")
-    ts_(T.l2[:, :], T.im16[:, :], T.pm[:, :], A.is_equal, name="cst")
-    ts_(T.mq[:, :], T.im8[:, :], T.pg[:, :], A.is_equal, name="cst")
-
-    def prep(s, e, name):
-        a, b = 8 * s, 8 * e
-        ts_(T.lo[:, a:b], T.li[:, a:b], 15, A.bitwise_and)
-        ts_(T.hi[:, a:b], T.li[:, a:b], 4, A.arith_shift_right)
-        vsync()
-        cp(T.lof[:, a:b], T.lo[:, a:b], name)
-        ts_(T.hic[:, a:b], T.hi[:, a:b], float(256 * rank - 1), A.subtract, 0.0, A.max)
-        vsync()
-        if s > 0:
-            ts_(T.hiu[:, a:b], T.hic[:, a:b], 257.0, A.min)
-
-    def onehots(s):
-        for q in range(8):
-            c = 8 * s + q
-            ts_(T.ohl[:, 128 * c:128 * c + 128], T.im16[:, :], T.lof[:, c:c + 1], A.is_equal, T.ev[:, q:q + 1], A.mult, "oh%d" % s)
-            ts_(T.ohr[:, 256 * c:256 * c + 256], T.i256[:, :], T.hic[:, c:c + 1], A.is_equal, name="oh%d" % s)
-
-    def table(s):
-        p = T["p%d" % s][:, 0:256]
-        out = T["tw%d" % s][:, 1:257]
-        V.wait_ge(sem["pt%d" % s], 8)
-        if s == 0:
-            cp(out, p)
-            return
-        a = 256 * (s - 1)
-        ts_(T.tu[:, a:a + 256], p, 0.0, A.is_gt, float(SLOT * s), A.mult)
-        vsync()
-        tt(T.tv[:, a:a + 256], T.tu[:, a:a + 256], p, A.add)
-        vsync()
-        tt(out, T.tv[:, a:a + 256], T["tw%d" % (s - 1)][:, 1:257], A.max)
-
-    def lookup(s):
-        c = 128 * (s - 1)
-        cp(T.gt[:, c:c + 128], T["tw%d" % (s - 1)][:, 0:258].indirect(T.hiu[:, 8 * s:8 * s + 8]))
-
-    V.wait_ge(sem.ldl, 128)
-    prep(0, 1, "vs")
-    vsync()
-    onehots(0)
-    V.wait_ge(sem.l1, 8)
-    V.wait_ge(sem.l2, 8)
-    prep(1, 3, "prep")
-    vsync()
-    onehots(1)
-    onehots(2)
-    table(0)
-    V.wait_ge(sem.cl, 1)
-    ts_(T.msk[:, 0:256], T.cl[:, 0:256], T.pm[:, :], A.is_equal)
-    vsync()
-    lookup(1)
-    table(1)
-    vsync()
-    lookup(2)
-    vsync()
-    tt(T.xt[:, 0:256], T.gt[:, 0:256], T.msk[:, 0:256], A.mult, "xt")
-    table(2)
-    V.wait_ge(sem.m1, 2)
-    tt(T.r2[:, 0:64], T.o1[:, 0:64], T.mq[:, :], A.mult, "r2")
-    tt(T.r2[:, 64:128], T.o1[:, 64:128], T.mq[:, :], A.mult, "r2")
-    V.wait_ge(sem.l3, 8)
-    prep(3, 4, "prepd")
-    vsync()
-    lookup(3)
-    onehots(3)
-    V.wait_ge(sem.m2, 1)
-    cp(T.off[:, 0:128], T.o2[:, 0:128], "of")
-    V.wait_ge(sem.cld, 1)
-    ts_(T.msk[:, 256:384], T.cld[:, 0:128], T.pm[:, :], A.is_equal)
-    vsync()
-    tt(T.xt[:, 256:384], T.gt[:, 256:384], T.msk[:, 256:384], A.mult, "xtd")
-    table(3)
-    V.wait_ge(sem.m1d, 1)
-    tt(T.r2[:, 128:192], T.o1[:, 128:192], T.mq[:, :], A.mult, "r2d")
-    vsync()
+    vq = vector_queue(g, T)
+    sync, fill, ts, tt, cp = vq
+    fill(T.gb[:, 1024:SLOT], "pad")
+    fill(T.win[:, 0:W0])
+    constants(g, T, vq, "rank")
+    g.wait_ge(sem.loc, noff + 4 + 12)
+    V.wait_ge(sem.lst, noff)
+    index_list(g, T, vq, rank, 3)
+    tabs = [T.tin[:, TB * s:TB * s + 264] for s in range(3)]
+    his = [T.tin[:, TB * s + 264:TB * s + 272] for s in (1, 2)] + [T.tb[:, 264:272]]
+    V.wait_ge(sem.tin, 3 * 8)
+    for s in (1, 2, 3):
+        ts(T.hiu[:, 8 * s:8 * s + 8], his[s - 1], 257.0, A.min)
+    tt(T.tw1[:, :], tabs[0], tabs[1], A.max)
+    sync()
+    tt(T.tw2[:, :], T.tw1[:, :], tabs[2], A.max)
+    for s, w in ((1, T.tin), (2, T.tw1), (3, T.tw2)):
+        if s == 3:
+            sync()
+        cp(T.gt[:, 128 * s - 128:128 * s], w[:, 0:258].indirect(T.hiu[:, 8 * s:8 * s + 8]))
+    V.wait_ge(sem.mkin, 2 * noff + 8)
+    sync()
+    tt(T.xt[:, :], T.gt[:, :], T.mkin[:, :], A.mult, "xt")
+    tt(T.tw3[:, :], T.tw2[:, :], T.tb[:, 0:264], A.max)
+    sync()
     cp(T.pos[:, :], T.tw3[:, 1:257])
-    V.wait_ge(sem.m2d, 1)
-    cp(T.off[:, 128:192], T.o2[:, 128:192])
-    vsync()
+    P.wait_ge(sem.cst, 3)
+    P.wait_ge(sem.xt, 1)
+    for s in range(3):
+        P.matmul(T.o1[:, 64 * s:64 * s + 64], T.xt[:, 128 * s:128 * s + 128], T.ee[:, :], True, True).then_inc(sem.m1, 1)
+    V.wait_ge(sem.m1, 3)
+    tt(T.r2[:, :], T.o1[:, 0:192], T.mq[:, :], A.mult, "r2")
+    P.wait_ge(sem.r2, 1)
+    P.matmul(T.o2[:, 0:192], T.l2[:, :], T.r2[:, :], True, True).then_inc(sem.m2, 1)
+    V.wait_ge(sem.m2, 1)
+    cp(T.off[:, :], T.o2[:, 0:192])
+    sync()
 
-    near = 4 * NON + 4 * (len(mates) - 1) * NOFF
-    other = 4 * len(mates) * NOFF
+    peers = 4 * (len(mates) - 1)
+    h = noff // 2
 
     def merge(s, name):
         a = W0 + SLOT * s
         tt(T.win[:, a:a + 1024], T.win[:, Z:a].indirect(T.off[:, 64 * (s - 1):64 * s]), T.win[:, a:a + 1024], A.add, name)
 
-    V.wait_ge(sem.v01, near + other)
+    V.wait_ge(sem.v01, 4 * NON + (peers + 4 * len(mates)) * h)
     merge(1, "vs")
-    V.wait_ge(sem.v2, near)
-    vsync()
+    V.wait_ge(sem.v2, 4 * NON + peers * noff)
+    sync()
     merge(2, "vs")
-    V.wait_ge(sem.v3, other)
-    vsync()
+    V.wait_ge(sem.v3, 4 * len(mates) * noff)
+    sync()
     merge(3, "mrg")
-    vsync()
+    sync()
     end = W0 + 4 * SLOT
-
-    def src(b):
-        return T.win[:, Z:end].indirect(T.pos[:, 32 * b:32 * b + 32])
-
-    for b in range(0, NB, 2):
-        V.tensor_copy(out=T.yb[:, BW * b:BW * b + BW], in_=src(b)).then_inc(sem["yd%d" % b], 1)
-
-    S.wait_ge(sem.cst, 5)
-    S.wait_ge(sem.prep, 1)
-    for n in range(16):
-        S.activation(out=T.rm[:, 16 * n:16 * n + 16], in_=T.ma[:, :], func=F.Copy, scale=T.lof[:, 8 + n:9 + n]).then_inc(sem.rm, 1)
-    S.wait_ge(sem.prepd, 1)
-    for n in range(16, 24):
-        S.activation(out=T.rm[:, 16 * n:16 * n + 16], in_=T.ma[:, :], func=F.Copy, scale=T.lof[:, 8 + n:9 + n]).then_inc(sem.rmd, 1)
     S.wait_ge(sem.mrg, 1)
-    for b in range(1, NB, 2):
-        S.activation(out=T.yb[:, BW * b:BW * b + BW], in_=src(b), func=F.Copy).then_inc(sem["yd%d" % b], 1)
-
-    def positions(s):
-        P.wait_ge(sem["oh%d" % s], 16)
-        for q in range(8):
-            c = 8 * s + q
-            P.matmul(T["p%d" % s][:, 0:256], T.ohl[:, 128 * c:128 * c + 128], T.ohr[:, 256 * c:256 * c + 256],
-                     q == 0, q == 7).then_inc(sem["pt%d" % s], 1)
-
-    P.wait_ge(sem.cst, 5)
-    positions(0)
-    P.wait_ge(sem.rm, 16)
-    P.matmul(T.cl[:, 0:256], T.bk[:, :], T.rm[:, 0:256], True, True).then_inc(sem.cl, 1)
-    positions(1)
-    positions(2)
-    P.wait_ge(sem.xt, 1)
-    for s in range(2):
-        P.matmul(T.o1[:, 64 * s:64 * s + 64], T.xt[:, 128 * s:128 * s + 128], T.ee[:, :], True, True).then_inc(sem.m1, 1)
-    P.wait_ge(sem.r2, 2)
-    P.matmul(T.o2[:, 0:128], T.l2[:, :], T.r2[:, 0:128], True, True).then_inc(sem.m2, 1)
-    P.wait_ge(sem.rmd, 8)
-    P.matmul(T.cld[:, 0:128], T.bk[:, :], T.rm[:, 256:384], True, True).then_inc(sem.cld, 1)
-    positions(3)
-    P.wait_ge(sem.xtd, 1)
-    P.matmul(T.o1[:, 128:192], T.xt[:, 256:384], T.ee[:, :], True, True).then_inc(sem.m1d, 1)
-    P.wait_ge(sem.r2d, 1)
-    P.wait_ge(sem.of, 1)
-    P.matmul(T.o2[:, 128:192], T.l2[:, :], T.r2[:, 128:192], True, True).then_inc(sem.m2d, 1)
-
-    for b in range(NB):
+    a = 0
+    for b, w in enumerate(BLOCKS):
+        src = T.win[:, Z:end].indirect(T.pos[:, a // 16:(a + w) // 16])
+        out = T.yb[:, a:a + w]
+        if b % 2 == 0:
+            V.tensor_copy(out=out, in_=src).then_inc(sem["yd%d" % b], 1)
+        else:
+            S.activation(out=out, in_=src, func=F.Copy).then_inc(sem["yd%d" % b], 1)
         Q.wait_ge(sem["yd%d" % b], 1)
-        Q.dma_start(T.y[:, BW * b:BW * b + BW], T.yb[:, BW * b:BW * b + BW]).then_inc(sem.st, 16)
-    Q.wait_ge(sem.st, 16 * NB)
+        Q.dma_start(T.y[:, a:a + w], out).then_inc(sem.st, 16)
+        a += w
+    Q.wait_ge(sem.st, 16 * len(BLOCKS))

from concourse.bass import DstId, RemoteDMATransfer
from concourse.mybir import AluOpType as A, AxisListType, ActivationFunctionType as F

NPIECE = 12
PW = 86
SLOT = NPIECE * PW
W0 = 8
Z = W0 - 1
BLOCKS = [256, 256, 512, 512, 640, 640, 640, 640]
NON = 4
TB = 272
QS = 6

SCRATCH = {
    "gb": ("sbuf", [128, SLOT], "float32"),
    "win": ("sbuf", [128, W0 + 4 * SLOT], "float32"),
    "yb": ("sbuf", [128, 4096], "float32"),
    "tin": ("sbuf", [128, 3 * TB], "float32"),
    "mkin": ("sbuf", [128, 384], "bfloat16"),
    "hiu": ("sbuf", [128, 32], "uint16"),
    "ee": ("sbuf", [128, 64], "float32"),
    "l2": ("sbuf", [128, 128], "float32"),
    "im8": ("sbuf", [128, 192], "bfloat16"),
    "mq": ("sbuf", [128, 192], "float32"),
    "gt": ("sbuf", [128, 384], "float32"),
    "xt": ("sbuf", [128, 384], "float32"),
    "r2": ("sbuf", [128, 192], "float32"),
    "off": ("sbuf", [128, 192], "uint16"),
    "tw1": ("sbuf", [128, 264], "float32"),
    "tw2": ("sbuf", [128, 264], "float32"),
    "tw3": ("sbuf", [128, 264], "float32"),
    "pos": ("sbuf", [128, 256], "uint16"),
    "li": ("sbuf", [128, 16], "int32"),
    "hi": ("sbuf", [128, 8], "int32"),
    "lo": ("sbuf", [128, 8], "int32"),
    "lof": ("sbuf", [128, 8], "float32"),
    "tb": ("sbuf", [128, TB], "float32"),
    "tu": ("sbuf", [128, 256], "float32"),
    "ohr": ("sbuf", [128, 8 * 256], "float16"),
    "ohl": ("sbuf", [128, 8 * 128], "float16"),
    "ab": ("sbuf", [128, 2 * 256], "bfloat16"),
    "lom": ("sbuf", [128, 8], "int32"),
    "lomf": ("sbuf", [128, 8], "float32"),
    "rm": ("sbuf", [128, 128], "bfloat16"),
    "mk": ("sbuf", [128, 128], "bfloat16"),
    "i256": ("sbuf", [128, 256], "bfloat16"),
    "im16": ("sbuf", [128, 128], "bfloat16"),
    "id16": ("sbuf", [128, 128], "bfloat16"),
    "ip": ("sbuf", [128, 1], "int32"),
    "ie": ("sbuf", [128, 8], "int32"),
    "pmi": ("sbuf", [128, 1], "int32"),
    "pgi": ("sbuf", [128, 1], "int32"),
    "pm": ("sbuf", [128, 1], "float32"),
    "pg": ("sbuf", [128, 1], "float32"),
    "pg112": ("sbuf", [128, 1], "float32"),
    "ev": ("sbuf", [128, 8], "float32"),
    "ma": ("sbuf", [128, 16], "bfloat16"),
    "bk": ("sbuf", [128, 128], "bfloat16"),
    "rsb": ("sbuf", [128, 3 * 88], "float32"),
    "s1": ("sbuf", [128, 88], "float32"),
    "sm": ("sbuf", [128, 88], "float32"),
    "cb": ("sbuf", [128, 88], "float32"),
    "pp": ("psum", [128, 512], "float32"),
    "cl": ("psum", [128, 512], "float32"),
    "o1": ("psum", [128, 512], "float32"),
    "o2": ("psum", [128, 512], "float32"),
}
SEMAPHORES = (["loc", "ldl", "ldg", "gi", "pad", "cst", "vs", "prep", "prepm", "rm", "cl", "xt", "m1", "r2", "m2", "mrg", "st",
               "lst", "lst2", "tin", "mkin", "tab", "tabm", "oha", "ohb", "abs", "ohs", "pt", "v01", "v2", "v3", "rs", "sum",
               "cab"] + ["yd%d" % b for b in range(len(BLOCKS))])


def engines(mask):
    return [b for b in range(16) if mask >> b & 1]


def bits(es):
    return sum(1 << b for b in es)


_PLAN = {}


def plan(T, topo):
    if not _PLAN:
        cores = list(T.cores)
        spot = {(topo.host(c), topo.chip(c)): [] for c in cores}
        for c in range(128 * 4):
            if (topo.host(c), topo.chip(c)) in spot:
                spot[topo.host(c), topo.chip(c)].append(c)
        helpers, indexers = [], []
        for c in cores:
            on = spot[topo.host(c), topo.chip(c)]
            hs = [[x for x in on[2 * u:2 * u + 2] if x not in cores][0] for u in range(len(on) // 2)]
            helpers.append(hs)
            indexers.append([x for x in on if x not in hs and x not in cores])
        _PLAN["h"], _PLAN["x"] = helpers, indexers
    return _PLAN["h"], _PLAN["x"]


def vector_queue(g, T):
    V, sem = g.vector, T.sem
    issued, waited = {}, {}

    def note(ins, name):
        ins.then_inc(sem[name], 1)
        issued[name] = issued.get(name, 0) + 1

    def sync():
        for n in issued:
            if waited.get(n, 0) < issued[n]:
                V.wait_ge(sem[n], issued[n])
                waited[n] = issued[n]

    def fill(ap, name="vs"):
        note(V.memset(ap, 0.0), name)

    def ts(out, in0, s1, op0, s2=None, op1=None, name="vs"):
        if op1 is None:
            note(V.tensor_scalar(out=out, in0=in0, scalar1=s1, scalar2=None, op0=op0), name)
        else:
            note(V.tensor_scalar(out=out, in0=in0, scalar1=s1, scalar2=s2, op0=op0, op1=op1), name)

    def tt(out, in0, in1, op, name="vs"):
        note(V.tensor_tensor(out=out, in0=in0, in1=in1, op=op), name)

    def cp(out, in_, name="vs"):
        note(V.tensor_copy(out=out, in_=in_), name)

    return sync, fill, ts, tt, cp


RAMPS = {"ip": ([[0, 1]], 0, 1), "ie": ([[16, 8]], 1, 1), "im16": ([[0, 8], [1, 16]], 0, 0), "i256": ([[1, 256]], 1, 0),
         "id16": ([[1, 8], [0, 16]], 0, 0), "im8": ([[0, 24], [1, 8]], 0, 0)}
KIND = {"rank": (["ip", "im16", "ie", "i256", "id16", "im8"], ["ee", "l2", "mq"]),
        "index": (["ip", "im16", "ie", "i256"], []),
        "both": (["ip", "im16", "ie", "i256", "id16"], ["ma", "bk"]),
        "mask": (["ip", "im16", "id16"], ["ma", "bk"])}


def constants(g, T, vq, kind):
    sync, fill, ts, tt, cp = vq
    ramps, consts = KIND[kind]
    for n in ramps:
        g.iota(T[n][:, :], *RAMPS[n], allow_small_or_imprecise_dtypes=True).then_inc(T.sem.gi, 1)
    if kind != "mask":
        fill(T.tb[:, 0:1])
        fill(T.tb[:, 257:264])
    g.vector.wait_ge(T.sem.gi, len(ramps))
    ts(T.pmi[:, :], T.ip[:, :], 15, A.bitwise_and)
    ts(T.pgi[:, :], T.ip[:, :], 4, A.arith_shift_right)
    sync()
    cp(T.pm[:, :], T.pmi[:, :])
    cp(T.pg[:, :], T.pgi[:, :])
    if kind != "mask":
        ts(T.pg112[:, :], T.pgi[:, :], 112.0, A.mult)
    sync()
    if kind != "mask":
        ts(T.ev[:, :], T.ie[:, :], T.pg112[:, :], A.add)
    make = {"ma": (T.im16[:, 0:16], T.pm),
            "bk": (T.id16[:, :], T.pg),
            "ee": (T.id16[:, 0:128:2], T.pg),
            "l2": (T.im16[:, :], T.pm),
            "mq": (T.im8[:, :], T.pg)}
    for n in consts:
        ts(T[n][:, :], make[n][0], make[n][1][:, :], A.is_equal, name="cst")
    sync()


def mask_list(g, T, vq, L):
    sync, fill, ts, tt, cp = vq
    V, S, P, sem = g.vector, g.scalar, g.tensor, T.sem
    ts(T.lom[:, :], L, 15, A.bitwise_and)
    sync()
    cp(T.lomf[:, :], T.lom[:, :], "prepm")
    S.wait_ge(sem.cst, 2)
    S.wait_ge(sem.prepm, 1)
    for q in range(8):
        S.activation(out=T.rm[:, 16 * q:16 * q + 16], in_=T.ma[:, :], func=F.Copy, scale=T.lomf[:, q:q + 1]).then_inc(sem.rm, 1)
    P.wait_ge(sem.cst, 2)
    P.wait_ge(sem.rm, 8)
    P.matmul(T.cl[:, 0:128], T.bk[:, :], T.rm[:, :], True, True).then_inc(sem.cl, 1)
    V.wait_ge(sem.cl, 1)
    ts(T.mk[:, :], T.cl[:, 0:128], T.pm[:, :], A.is_equal, name="tabm")
    sync()


def index_list(g, T, vq, rank, slot):
    sync, fill, ts, tt, cp = vq
    V, S, P, sem = g.vector, g.scalar, g.tensor, T.sem
    L, hic = T.li[:, 8:16], T.tb[:, 264:272]
    ts(T.hi[:, :], L, 4, A.arith_shift_right)
    ts(T.lo[:, :], L, 15, A.bitwise_and)
    sync()
    ts(hic, T.hi[:, :], float(256 * rank - 1), A.subtract, 0.0, A.max, "prep")
    cp(T.lof[:, :], T.lo[:, :])
    sync()

    def hot(q):
        return T.ohr[:, 256 * q:256 * q + 256]

    for q in range(8):
        n = "oha" if q < 4 else "ohb"
        ts(T.ohl[:, 128 * q:128 * q + 128], T.im16[:, :], T.lof[:, q:q + 1], A.is_equal, T.ev[:, q:q + 1], A.mult, n)
        if q < QS:
            ts(hot(q), T.i256[:, :], T.tb[:, 264 + q:265 + q], A.is_equal, name=n)
    S.wait_ge(sem.prep, 1)
    for q in range(QS, 8):
        a = 256 * (q - QS)
        S.activation(out=T.ab[:, a:a + 256], in_=T.i256[:, :], func=F.Abs, bias=T.tb[:, 264 + q:265 + q], scale=-1.0).then_inc(sem.abs, 1)
    S.wait_ge(sem.abs, 8 - QS)
    for q in range(QS, 8):
        a = 256 * (q - QS)
        S.activation(out=hot(q), in_=T.ab[:, a:a + 256], func=F.Relu, bias=1.0, scale=-1.0).then_inc(sem.ohs, 1)

    def mm(q):
        P.matmul(T.pp[:, 0:256], T.ohl[:, 128 * q:128 * q + 128], hot(q), q == 0, q == 7).then_inc(sem.pt, 1)

    P.wait_ge(sem.oha, 8)
    for q in range(4):
        mm(q)
    P.wait_ge(sem.ohb, 4 + QS - 4)
    for q in range(4, QS):
        mm(q)
    P.wait_ge(sem.ohs, 8 - QS)
    for q in range(QS, 8):
        mm(q)
    V.wait_ge(sem.pt, 8)
    if slot == 0:
        cp(T.tb[:, 1:257], T.pp[:, 0:256], "tab")
    else:
        ts(T.tu[:, :], T.pp[:, 0:256], 0.0, A.is_gt, float(SLOT * slot), A.mult)
        sync()
        tt(T.tb[:, 1:257], T.tu[:, :], T.pp[:, 0:256], A.add, "tab")
    sync()


def rank_program(g, core, T, topo):
    cores = list(T.cores)
    helpers, indexers = plan(T, topo)
    hosts = [topo.host(c) for c in cores]

    def here(r, hst):
        return [q for q in range(len(cores)) if hosts[q] == hst and topo.chip(cores[q]) == topo.chip(cores[r])][0]

    def rack_peer(r):
        return [here(r, h) for h in sorted(set(hosts)) if h != hosts[r] and topo.rack(h) == topo.rack(hosts[r])][0]

    def cable_peer(r):
        return [q for q in (here(r, h) for h in sorted(set(hosts)) if topo.rack(h) != topo.rack(hosts[r]))
                if topo.may_write(cores[r], cores[q])][0]

    def dst(d):
        rid, pid = topo.addr(d, core)
        return DstId(rid=rid, pnc=pid)

    def xfer(src, pairs, es, sem):
        return RemoteDMATransfer(dst_ids=[dst(d) for d, _ in pairs], dma_engine_mask=bits(es), remote_sem=sem,
                                 srcs=[src], dsts=[ap for _, ap in pairs], alu_op=0)

    sem = T.sem
    rank = T.rank_of(core)
    if rank is not None:
        mates = [r for r in range(len(cores)) if hosts[r] == hosts[rank]]
        run_rank(g, core, rank, mates, rack_peer(rank), cable_peer(rank), helpers, indexers, T, topo, xfer)
        return
    vq = vector_queue(g, T)
    sync, fill, ts, tt, cp = vq

    def send(ts_):
        g.remote_dma_fused(ts_, local_sem=sem.loc)

    own = [(r, u) for r in range(len(cores)) for u in range(4) if helpers[r][u] == core]
    idx = [(r, s) for r in range(len(cores)) for s in range(3) if indexers[r][s] == core]
    if idx:
        r, s = idx[0]
        R = rack_peer(r)
        es = engines(topo.mask(core, cores[r]))
        noff = len(engines(topo.mask(core, cores[R])))
        constants(g, T, vq, "index" if s else "both")
        g.vector.wait_ge(sem.lst, noff if s else 4)
        index_list(g, T, vq, r, s)
        g.wait_ge(sem.tab, 1)
        g.wait_ge(sem.prep, 1)
        send([xfer(T.tb[:, :], [(cores[r], T.tin[:, TB * s:TB * s + TB])], es[:8], sem.tin)])
        if s == 0:
            g.vector.wait_ge(sem.lst2, noff)
            mask_list(g, T, vq, T.li[:, 0:8])
            g.wait_ge(sem.tabm, 1)
            send([xfer(T.mk[:, :], [(cores[r], T.mkin[:, 128:256])], es[:8], sem.mkin)])
        g.wait_ge(sem.loc, 8 if s else 16)
        return
    if not own:
        return
    r, u = own[0]
    mates = [q for q in range(len(cores)) if hosts[q] == hosts[r]]
    others = [q for q in range(len(cores)) if topo.rack(hosts[q]) == topo.rack(hosts[r]) and q not in mates]
    k = 4 * mates.index(r) + u
    R, C = rack_peer(r), cable_peer(r)
    off_es = engines(topo.mask(core, cores[R]))
    on_es = [e for e in engines(topo.mask(core, cores[r])) if e not in off_es]
    noff = len(off_es)
    L = T.li[:, 8:16]

    if u == 3:
        g.wait_ge(sem.lst, noff)
        send([xfer(L, [(cores[R], L)], off_es, sem.lst)])
    elif u == 1:
        g.wait_ge(sem.lst, 4)
        send([xfer(L, [(indexers[C][0], T.li[:, 0:8])], off_es, sem.lst2)])
    else:
        constants(g, T, vq, "mask")
        g.vector.wait_ge(sem.lst, 4 if u == 0 else noff)
        mask_list(g, T, vq, L)
        g.wait_ge(sem.tabm, 1)
        send([xfer(T.mk[:, :], [(cores[R], T.mkin[:, 128 * u:128 * u + 128])], off_es, sem.mkin)])
    g.vector.wait_ge(sem.rs, 3)
    tt(T.s1[:, 0:PW], T.rsb[:, 0:PW], T.rsb[:, 88:88 + PW], A.add)
    sync()
    tt(T.sm[:, 0:PW], T.s1[:, 0:PW], T.rsb[:, 176:176 + PW], A.add, "sum")
    g.wait_ge(sem.sum, 1)

    def at(slot):
        a = W0 + SLOT * slot + PW * k
        return T.win[:, a:a + PW]

    S = T.sm[:, 0:PW]
    h = noff // 2
    send([xfer(S, [(helpers[C][u], T.cb[:, 0:PW])], off_es[:h], sem.cab),
          xfer(S, [(cores[q], at(0)) for q in mates if q != r] + [(cores[q], at(1)) for q in others], off_es[h:], sem.v01),
          xfer(S, [(cores[r], at(0))], on_es[:NON], sem.v01)])
    g.wait_ge(sem.cab, h)
    B = T.cb[:, 0:PW]
    send([xfer(B, [(cores[q], at(2)) for q in mates if q != r], off_es, sem.v2),
          xfer(B, [(cores[r], at(2))], on_es[:NON], sem.v2)])
    send([xfer(B, [(cores[q], at(3)) for q in others], off_es, sem.v3)])
    g.wait_ge(sem.loc, 4 * noff + 2 * NON)


def run_rank(g, core, rank, mates, R, C, helpers, indexers, T, topo, xfer):
    sem = T.sem
    V, S, P, Q = g.vector, g.scalar, g.tensor, g.sync
    hs = helpers[rank]
    far = [h for q in mates if q != rank for h in helpers[q]]
    off_es = engines(topo.mask(core, far[0]))
    on_es = [e for e in engines(topo.mask(core, hs[0])) if e not in off_es]
    noff = len(off_es)
    for i in range(8):
        (Q if i < 4 else S).dma_start(T.li[16 * i:16 * i + 16, 0:8], T.idx[:, 8 * i:8 * i + 8]).then_inc(sem.ldl, 16)
    Q.dma_start(T.gb[:, 0:1024], T.g[:, :]).then_inc(sem.ldg, 16)

    g.wait_ge(sem.ldl, 128)
    L = T.li[:, 0:8]

    def to(cs):
        return [(c, T.li[:, 8:16]) for c in cs]

    g.remote_dma_fused([xfer(L, to([helpers[C][3], indexers[R][1], indexers[C][2], helpers[C][2]]), off_es, sem.lst),
                        xfer(L, to([hs[1], hs[0], indexers[rank][0]]), on_es[0:4], sem.lst)], local_sem=sem.loc)
    g.wait_ge(sem.ldg, 16)
    g.wait_ge(sem.pad, 1)
    ts_, i_off, i_on = [], 0, 0
    me = mates.index(rank)
    for m, q in enumerate(mates):
        for u in range(4):
            k = 4 * m + u
            if q == rank:
                e, i_on = on_es[i_on], i_on + 1
            else:
                e, i_off = off_es[i_off], i_off + 1
            ts_.append(xfer(T.gb[:, PW * k:PW * k + PW], [(helpers[q][u], T.rsb[:, 88 * me:88 * me + PW])], [e], sem.rs))
    g.remote_dma_fused(ts_, local_sem=sem.loc)

    vq = vector_queue(g, T)
    sync, fill, ts, tt, cp = vq
    fill(T.gb[:, 1024:SLOT], "pad")
    fill(T.win[:, 0:W0])
    constants(g, T, vq, "rank")
    g.wait_ge(sem.loc, noff + 4 + 12)
    V.wait_ge(sem.lst, noff)
    index_list(g, T, vq, rank, 3)
    tabs = [T.tin[:, TB * s:TB * s + 264] for s in range(3)]
    his = [T.tin[:, TB * s + 264:TB * s + 272] for s in (1, 2)] + [T.tb[:, 264:272]]
    V.wait_ge(sem.tin, 3 * 8)
    for s in (1, 2, 3):
        ts(T.hiu[:, 8 * s:8 * s + 8], his[s - 1], 257.0, A.min)
    tt(T.tw1[:, :], tabs[0], tabs[1], A.max)
    sync()
    tt(T.tw2[:, :], T.tw1[:, :], tabs[2], A.max)
    for s, w in ((1, T.tin), (2, T.tw1), (3, T.tw2)):
        if s == 3:
            sync()
        cp(T.gt[:, 128 * s - 128:128 * s], w[:, 0:258].indirect(T.hiu[:, 8 * s:8 * s + 8]))
    V.wait_ge(sem.mkin, 2 * noff + 8)
    sync()
    tt(T.xt[:, :], T.gt[:, :], T.mkin[:, :], A.mult, "xt")
    tt(T.tw3[:, :], T.tw2[:, :], T.tb[:, 0:264], A.max)
    sync()
    cp(T.pos[:, :], T.tw3[:, 1:257])
    P.wait_ge(sem.cst, 3)
    P.wait_ge(sem.xt, 1)
    for s in range(3):
        P.matmul(T.o1[:, 64 * s:64 * s + 64], T.xt[:, 128 * s:128 * s + 128], T.ee[:, :], True, True).then_inc(sem.m1, 1)
    V.wait_ge(sem.m1, 3)
    tt(T.r2[:, :], T.o1[:, 0:192], T.mq[:, :], A.mult, "r2")
    P.wait_ge(sem.r2, 1)
    P.matmul(T.o2[:, 0:192], T.l2[:, :], T.r2[:, :], True, True).then_inc(sem.m2, 1)
    V.wait_ge(sem.m2, 1)
    cp(T.off[:, :], T.o2[:, 0:192])
    sync()

    peers = 4 * (len(mates) - 1)
    h = noff // 2

    def merge(s, name):
        a = W0 + SLOT * s
        tt(T.win[:, a:a + 1024], T.win[:, Z:a].indirect(T.off[:, 64 * (s - 1):64 * s]), T.win[:, a:a + 1024], A.add, name)

    V.wait_ge(sem.v01, 4 * NON + (peers + 4 * len(mates)) * h)
    merge(1, "vs")
    V.wait_ge(sem.v2, 4 * NON + peers * noff)
    sync()
    merge(2, "vs")
    V.wait_ge(sem.v3, 4 * len(mates) * noff)
    sync()
    merge(3, "mrg")
    sync()
    end = W0 + 4 * SLOT
    S.wait_ge(sem.mrg, 1)
    a = 0
    for b, w in enumerate(BLOCKS):
        src = T.win[:, Z:end].indirect(T.pos[:, a // 16:(a + w) // 16])
        out = T.yb[:, a:a + w]
        if b % 2 == 0:
            V.tensor_copy(out=out, in_=src).then_inc(sem["yd%d" % b], 1)
        else:
            S.activation(out=out, in_=src, func=F.Copy).then_inc(sem["yd%d" % b], 1)
        Q.wait_ge(sem["yd%d" % b], 1)
        Q.dma_start(T.y[:, a:a + w], out).then_inc(sem.st, 16)
        a += w
    Q.wait_ge(sem.st, 16 * len(BLOCKS))
